import numpy as np
import ml_dtypes


def mxq(x, axis, fmt="e4m3"):
    dtype, down = {"e4m3": (ml_dtypes.float8_e4m3fn, 7), "e5m2": (ml_dtypes.float8_e5m2, 14)}[fmt]
    v = np.moveaxis(np.asarray(x, np.float32).astype(ml_dtypes.bfloat16).astype(np.float64), axis, -1)
    blocks = v.reshape(v.shape[:-1] + (-1, 32))
    amax = np.abs(blocks).max(-1, keepdims=True)
    byte = np.maximum(np.where(amax > 0, np.frexp(amax)[1] - 1 + 127, 0) - down, 1)
    scale = np.exp2(byte - 127.0)
    codes = (blocks / scale).astype(np.float32).astype(dtype).astype(np.float64)
    return np.moveaxis((codes * scale).reshape(v.shape), -1, axis)


WIDE = False


def mx_kscale(k):
    if not WIDE:
        return np.ones(k)
    levels = np.array([10, -10, 5, -5, 0])
    if k % 512:
        return np.exp2(np.random.permutation(np.resize(levels, k // 32))).repeat(32)
    a = np.empty((k // 512, 16))
    for p in range(k // 512):
        a[p, :8] = np.random.permutation(np.resize(levels, 8))
        for g in range(8):
            far = levels[np.abs(levels - a[p, g]) >= 10]
            a[p, g + 8] = far[np.random.randint(len(far))]
    return np.exp2(a.ravel()).repeat(32)


def f64(x):
    return np.asarray(x).astype(np.float64)


def striped(idx):
    return np.tile(idx.reshape(-1, 16).T, (8, 1)).astype(np.uint16)


def unstriped(offs):
    return offs[:16].T.reshape(-1).astype(np.int64)


def striped8(idx):
    return np.concatenate([x.reshape(-1, 16).T for x in idx]).astype(np.uint16)


def runs(offs, k):
    lists = np.stack([offs[16 * r : 16 * r + 16].T.reshape(-1) for r in range(8)]).astype(np.int64)
    return lists[np.arange(k) % 512 // 64]


def pack_weight(w):
    k, n = w.shape
    w = f64(np.asarray(w, np.float32).astype(ml_dtypes.bfloat16)).reshape(k // 32, 32, n)
    amax = np.abs(w).max(1)
    byte = np.clip(np.where(amax > 0, np.frexp(amax)[1] - 1 + 127 - 7, 1), 1, 254)
    scaled = (w * np.exp2(127.0 - byte)[:, None, :]).reshape(k, n).astype(np.float32)
    words = np.ascontiguousarray(scaled.reshape(k // 512, 128, 4, n).transpose(0, 1, 3, 2)).astype(ml_dtypes.float8_e4m3fn).view(np.uint8)
    return words, np.ascontiguousarray(byte.astype(np.uint8).reshape(k // 512, 16, n))


def unpack_weight(words, scales):
    g, p, n, _ = words.shape
    vals = np.ascontiguousarray(words).view(ml_dtypes.float8_e4m3fn).astype(np.float64) * np.repeat(np.exp2(scales.astype(np.float64) - 127.0), 8, axis=1)[..., None]
    return vals.transpose(0, 1, 3, 2).reshape(g * 512, n)


def sigmoid(v):
    return 1.0 / (1.0 + np.exp(-np.maximum(v, -700.0)))


K, T, S, N, H = 512, 2048, 512, 512, 512


def setup_inputs():
    n = np.random.standard_normal
    s = mx_kscale(K)[:, None]
    u = mx_kscale(S)
    packed_xT = pack_weight(n((K, T)) * s)
    return {
        "x_words": packed_xT[0],
        "x_scales": packed_xT[1],
        "wa": (n((K, H)) / np.sqrt(K) / s).astype(np.float32),
        "gt": (np.random.uniform(0.5, 1.5, (S, 1)) * u[:, None]).astype(np.float32),
        "w1": (n((S, N)) / np.sqrt(S) / u[:, None]).astype(np.float32),
        "offs": striped(np.random.permutation(T)[:S]),
        "n1": striped8(np.stack([np.random.permutation(H) for _ in range(8)])),
        "n2": striped8(np.stack([np.random.permutation(H) for _ in range(8)])),
        "n3": striped8(np.stack([np.random.permutation(H) for _ in range(8)])),
    }


def reference(x_words, x_scales, wa, gt, w1, offs, n1, n2, n3):
    xq = unpack_weight(x_words, x_scales)[:, unstriped(offs)]
    y = xq.T @ mxq(f64(wa), 0, "e4m3")
    pa = y[np.arange(S)[:, None], runs(n1, S)]
    kr = np.exp(-0.5 * ((y - pa) ** 2))
    pb = y[np.arange(S)[:, None], runs(n2, S)]
    kr2 = np.exp(-0.5 * ((y - pb) ** 2))
    z = f64(gt) * ((kr * pa + kr2 * pb) / (kr + kr2 + 0.5))
    h = mxq(f64(w1), 0, "e4m3").T @ mxq(z, 0, "e4m3")
    return h * (sigmoid(h[np.arange(N)[:, None], runs(n3, N)]))

@@ -1,0 +1,266 @@
+from contextlib import ExitStack
+
+import concourse.mybir as mybir
+
+K, T, S, N, H = 512, 2048, 512, 512, 512
+FLOPS = 2 * K * S * H + 2 * S * N * H
+
+F32 = mybir.dt.float32
+BF16 = mybir.dt.bfloat16
+I32 = mybir.dt.int32
+U32 = mybir.dt.uint32
+U16 = mybir.dt.uint16
+U8 = mybir.dt.uint8
+FP8X4 = mybir.dt.float8_e4m3fn_x4
+ACT = mybir.ActivationFunctionType
+ALU = mybir.AluOpType
+
+P = 128
+PACK = 4
+HALF = 256
+CHUNK = 128
+
+
+def tile_picked_tokkerngate_none_p_kernel(
+    tc, x_words, x_scales, wa, gt, w1, offs, n1, n2, n3, out
+):
+    nc = tc.nc
+    with ExitStack() as ctx:
+        keep = ctx.enter_context(tc.tile_pool(name="keep", bufs=1))
+        psum = ctx.enter_context(tc.psum_pool(name="psum", bufs=1))
+
+        def sb(name, shape, dtype):
+            return keep.tile(shape, dtype, name=name, align_bytes=64)
+
+        def load_list(name, src):
+            tile = keep.tile([P, 32], U16, name=name)
+            nc.sync.dma_start(tile[:], src)
+            return tile
+
+        def gather(engine, dst, window, lst, cols):
+            src = window[:].indirect(lst[:, cols.start // 16 : cols.stop // 16])
+            if engine == "vector":
+                nc.vector.tensor_copy(dst, src)
+            else:
+                nc.scalar.activation(dst, src, ACT.Copy)
+
+        xw = sb("xw", [P, T], I32)
+        nc.sync.dma_start(xw[:], x_words[0].rearrange("p n t -> p (n t)").bitcast(I32))
+        offs_t = load_list("offs_t", offs)
+        xs = sb("xs", [P, T], U8)
+        nc.vector.memset(xs[:].bitcast(I32), 0)
+        for q in range(4):
+            nc.scalar.dma_start(
+                xs[32 * q : 32 * q + 4, :].bitcast(I32), x_scales[0, 4 * q : 4 * q + 4, :].bitcast(I32)
+            )
+        wa_rows = wa.rearrange("(p j) c -> p j c", j=PACK)
+        wa_raw = []
+        for h in range(2):
+            raw = sb(f"wa_raw{h}", [P, PACK, HALF], F32)
+            nc.sync.dma_start(raw[:], wa_rows[:, :, h * HALF : (h + 1) * HALF])
+            wa_raw.append(raw)
+        n1_t = load_list("n1_t", n1)
+        n2_t = load_list("n2_t", n2)
+        w1_raw = sb("w1_raw", [P, PACK, N], F32)
+        nc.sync.dma_start(w1_raw[:], w1.rearrange("(p j) c -> p j c", j=PACK))
+        gt_t = sb("gt_t", [P, PACK], F32)
+        nc.sync.dma_start(gt_t[:], gt.rearrange("(p t) o -> p (t o)", t=PACK))
+        n3_t = load_list("n3_t", n3)
+
+        xg_s = sb("xg_s", [P, S], U8)
+        nc.vector.tensor_copy(xg_s[:].rearrange("p (t m) -> p m t", t=PACK), xs[:].indirect(offs_t[:]))
+        xg_w = sb("xg_w", [P, S], U32)
+        nc.vector.tensor_copy(
+            xg_w[:].rearrange("p (t m) -> p m t", t=PACK), xw[:].bitcast(U32).indirect(offs_t[:])
+        )
+
+        wa_q = [sb(f"wa_q{h}", [P, HALF], U32) for h in range(2)]
+        wa_s = [sb(f"wa_s{h}", [P, HALF], U8) for h in range(2)]
+
+        def cast_wa(engine, h, c0, width):
+            grouped = sb(f"wa_g{h}_{c0}", [P, width * PACK], BF16)
+            dst = grouped[:].rearrange("p (c i j) -> p c j i", i=4, j=PACK)
+            src = wa_raw[h][:, :, c0 : c0 + width].rearrange("p j (c i) -> p c j i", i=4)
+            if engine == "vector":
+                nc.vector.tensor_copy(dst, src)
+            else:
+                nc.scalar.copy(dst, src)
+            return grouped
+
+        def quant_wa(grouped, h, c0, width):
+            nc.vector.quantize_mx(
+                out=wa_q[h][:, c0 : c0 + width].bitcast(FP8X4), scales=wa_s[h][:, c0 : c0 + width], in_=grouped[:]
+            )
+
+        y_ps = [psum.tile([P, H], F32, name=f"y_ps{t}", tag=f"bank{t}") for t in range(PACK)]
+        y_sb = [sb(f"y_sb{t}", [P, H], F32) for t in range(PACK)]
+
+        def product_y(h):
+            cols = slice(h * HALF, (h + 1) * HALF)
+            for t in range(PACK):
+                rows = slice(t * P, (t + 1) * P)
+                nc.tensor.matmul_mx(
+                    out=y_ps[t][:, cols],
+                    lhsT=xg_w[:, rows].bitcast(FP8X4),
+                    lhsT_scale=xg_s[:, rows],
+                    rhs=wa_q[h][:].bitcast(FP8X4),
+                    rhs_scale=wa_s[h][:],
+                    start=True,
+                    stop=True,
+                )
+
+        def empty_y(engine, t, h):
+            cols = slice(h * HALF, (h + 1) * HALF)
+            if engine == "vector":
+                nc.vector.tensor_copy(y_sb[t][:, cols], y_ps[t][:, cols])
+            else:
+                nc.scalar.copy(y_sb[t][:, cols], y_ps[t][:, cols])
+
+        g0 = cast_wa("scalar", 0, 0, HALF)
+        quant_wa(g0, 0, 0, HALF)
+        g2 = cast_wa("vector", 1, 0, CHUNK)
+        g3 = cast_wa("scalar", 1, CHUNK, CHUNK)
+        product_y(0)
+        quant_wa(g2, 1, 0, CHUNK)
+        quant_wa(g3, 1, CHUNK, CHUNK)
+        for t in range(PACK):
+            empty_y("scalar", t, 0)
+        product_y(1)
+        empty_y("scalar", 0, 1)
+        empty_y("vector", 1, 1)
+
+        units = [(t, h) for h in range(2) for t in range(PACK)]
+        pick = [sb(f"pick{u}", [P, 2, HALF], F32) for u in range(8)]
+        diff = [sb(f"diff{u}", [P, 2, HALF], F32) for u in range(8)]
+        sq_pair = [sb(f"sq{v}", [P, PACK * HALF], F32) for v in range(4)]
+        sq = [sq_pair[u // 2][:, (u % 2) * 2 * HALF : (u % 2 + 1) * 2 * HALF] for u in range(8)]
+        kt = [sb(f"kt{u}", [P, 2, 2, HALF], F32) for u in range(8)]
+        both = [sb(f"both{h}", [P, PACK, 2, HALF], F32) for h in range(2)]
+
+        def fetch(u, engines):
+            t, h = units[u]
+            cols = slice(h * HALF, (h + 1) * HALF)
+            gather(engines[0], pick[u][:, 0, :], y_sb[t], n1_t, cols)
+            gather(engines[1], pick[u][:, 1, :], y_sb[t], n2_t, cols)
+
+        def subtract(u):
+            t, h = units[u]
+            cols = slice(h * HALF, (h + 1) * HALF)
+            nc.vector.tensor_tensor(
+                diff[u][:], pick[u][:], y_ps[t][:, cols].unsqueeze(1).to_broadcast([P, 2, HALF]), ALU.subtract
+            )
+
+        def weights(u):
+            nc.scalar.activation(sq[u], diff[u][:].rearrange("p a c -> p (a c)"), ACT.Square)
+            nc.scalar.activation(kt[u][:, 0].rearrange("p a c -> p (a c)"), sq[u], ACT.Exp, scale=-0.5)
+
+        def sums(u):
+            t, h = units[u]
+            nc.vector.scalar_tensor_tensor(
+                kt[u][:, 1].rearrange("p a c -> p (a c)"),
+                kt[u][:, 0].rearrange("p a c -> p (a c)"),
+                gt_t[:, t : t + 1],
+                pick[u][:].rearrange("p a c -> p (a c)"),
+                ALU.mult,
+                ALU.mult,
+            )
+            nc.vector.tensor_tensor(both[h][:, t], kt[u][:, :, 0, :], kt[u][:, :, 1, :], ALU.add)
+
+        w1_g = sb("w1_g", [P, N * PACK], BF16)
+        w1_q = sb("w1_q", [P, N], U32)
+        w1_s = sb("w1_s", [P, N], U8)
+
+        fetch(0, ("scalar", "scalar"))
+        fetch(1, ("vector", "vector"))
+        empty_y("vector", 2, 1)
+        empty_y("vector", 3, 1)
+        subtract(0)
+        fetch(2, ("scalar", "vector"))
+        subtract(1)
+        weights(0)
+        nc.vector.tensor_copy(
+            w1_g[:].rearrange("p (t m j) -> p m j t", t=PACK, j=PACK),
+            w1_raw[:].rearrange("p j (m t) -> p m j t", t=PACK),
+        )
+        for u in range(1, 8):
+            if u + 2 < 8:
+                fetch(u + 2, ("scalar", "vector" if u == 1 else "scalar"))
+            if u + 1 < 8:
+                subtract(u + 1)
+            weights(u)
+            sums(u - 1)
+            if u == 1:
+                nc.vector.quantize_mx(out=w1_q[:].bitcast(FP8X4), scales=w1_s[:], in_=w1_g[:])
+        sums(7)
+
+        h_ps = [
+            [psum.tile([P, H], F32, name=f"h_ps0_{t}", tag=f"bank{PACK + t}") for t in range(PACK)],
+            [psum.tile([P, H], F32, name=f"h_ps1_{t}", tag=f"bank{t}") for t in range(PACK)],
+        ]
+        gate = [sb(f"gate{t}", [P, H], F32) for t in range(PACK)]
+        roots = []
+        for c in range(4):
+            h, c0 = c // 2, (c % 2) * CHUNK
+            root = sq_pair[3 - h][:].rearrange("p (t c) -> p t c", t=PACK)[:, :, c0 : c0 + CHUNK]
+            nc.scalar.activation(root, both[h][:, :, 0, c0 : c0 + CHUNK], ACT.Abs_reciprocal_sqrt, bias=0.5)
+            roots.append(root)
+
+        def sigmoid_h(h, c0, width):
+            for t in range(PACK):
+                nc.scalar.activation(
+                    gate[t][:, h * HALF + c0 : h * HALF + c0 + width], h_ps[h][t][:, c0 : c0 + width], ACT.Sigmoid
+                )
+
+        def scale_once(c):
+            h, c0 = c // 2, (c % 2) * CHUNK
+            once = sb(f"once{c}", [P, PACK, CHUNK], F32)
+            nc.vector.tensor_tensor(once[:], both[h][:, :, 1, c0 : c0 + CHUNK], roots[c], ALU.mult)
+            return once
+
+        def scale_twice(c, once):
+            z = sb(f"z{c}", [P, CHUNK * PACK], BF16)
+            nc.vector.tensor_tensor(
+                z[:].rearrange("p (c i t) -> p c t i", i=4, t=PACK),
+                once[:].rearrange("p t (c i) -> p c t i", i=4),
+                roots[c].rearrange("p t (c i) -> p c t i", i=4),
+                ALU.mult,
+            )
+            return z
+
+        def product_h(c, z):
+            h, c0 = c // 2, (c % 2) * CHUNK
+            z_q = sb(f"z_q{c}", [P, CHUNK], U32)
+            z_s = sb(f"z_s{c}", [P, CHUNK], U8)
+            nc.vector.quantize_mx(out=z_q[:].bitcast(FP8X4), scales=z_s[:], in_=z[:])
+            for t in range(PACK):
+                rows = slice(t * P, (t + 1) * P)
+                nc.tensor.matmul_mx(
+                    out=h_ps[h][t][:, c0 : c0 + CHUNK],
+                    lhsT=w1_q[:, rows].bitcast(FP8X4),
+                    lhsT_scale=w1_s[:, rows],
+                    rhs=z_q[:].bitcast(FP8X4),
+                    rhs_scale=z_s[:],
+                    start=True,
+                    stop=True,
+                )
+
+        once = scale_once(0)
+        for c in range(4):
+            z = scale_twice(c, once)
+            if c + 1 < 4:
+                once = scale_once(c + 1)
+            product_h(c, z)
+            if c == 1:
+                sigmoid_h(0, 0, HALF)
+            if c >= 2:
+                sigmoid_h(1, (c - 2) * CHUNK, CHUNK)
+
+        out_rows = out.rearrange("(p t) c -> p t c", t=PACK)
+        for t in range(PACK):
+            for h in range(2):
+                cols = slice(h * HALF, (h + 1) * HALF)
+                fetched = sb(f"fetched{t}_{h}", [P, HALF], F32)
+                gather("vector" if t == 0 else "scalar", fetched[:], gate[t], n3_t, cols)
+                res = sb(f"res{t}_{h}", [P, HALF], F32)
+                nc.vector.tensor_tensor(res[:], h_ps[h][t][:, 0:HALF], fetched[:], ALU.mult)
+                nc.sync.dma_start(out_rows[:, t, cols], res[:])

@@ -1,6 +1,7 @@
 from contextlib import ExitStack
 
 import concourse.mybir as mybir
+from concourse.masks import make_identity
 
 K, T, S, N, H = 512, 2048, 512, 512, 512
 FLOPS = 2 * K * S * H + 2 * S * N * H
@@ -27,6 +28,7 @@ def tile_picked_tokkerngate_none_p_kernel(
     nc = tc.nc
     with ExitStack() as ctx:
         keep = ctx.enter_context(tc.tile_pool(name="keep", bufs=1))
+        reuse = ctx.enter_context(tc.tile_pool(name="reuse", bufs=1))
         psum = ctx.enter_context(tc.psum_pool(name="psum", bufs=1))
 
         def sb(name, shape, dtype):
@@ -37,28 +39,32 @@ def tile_picked_tokkerngate_none_p_kernel(
             nc.sync.dma_start(tile[:], src)
             return tile
 
-        def gather(engine, dst, window, lst, cols):
+        def gather(engine, dst, window, lst, cols, negate=False):
             src = window[:].indirect(lst[:, cols.start // 16 : cols.stop // 16])
-            if engine == "vector":
+            if engine == "vector" and negate:
+                nc.vector.tensor_scalar(dst, src, -1.0, 0.0, ALU.mult, ALU.add)
+            elif engine == "vector":
                 nc.vector.tensor_copy(dst, src)
             else:
-                nc.scalar.activation(dst, src, ACT.Copy)
+                nc.scalar.activation(dst, src, ACT.Copy, scale=-1.0 if negate else 1.0)
 
-        xw = sb("xw", [P, T], I32)
-        nc.sync.dma_start(xw[:], x_words[0].rearrange("p n t -> p (n t)").bitcast(I32))
+        wa_rows = wa.rearrange("(p j) c -> p j c", j=PACK)
+        wa_raw = [
+            sb("wa_raw0", [P, PACK, HALF], F32),
+            reuse.tile([P, PACK, HALF], F32, name="wa_raw1", offset=0),
+        ]
+        nc.sync.dma_start(wa_raw[0][:], wa_rows[:, :, 0:HALF])
         offs_t = load_list("offs_t", offs)
         xs = sb("xs", [P, T], U8)
-        nc.vector.memset(xs[:].bitcast(I32), 0)
+        nc.vector.memset(xs[:, 0 : T // 2].bitcast(I32), 0)
+        nc.gpsimd.memset(xs[:, T // 2 : T].bitcast(I32), 0)
         for q in range(4):
-            nc.scalar.dma_start(
+            nc.sync.dma_start(
                 xs[32 * q : 32 * q + 4, :].bitcast(I32), x_scales[0, 4 * q : 4 * q + 4, :].bitcast(I32)
             )
-        wa_rows = wa.rearrange("(p j) c -> p j c", j=PACK)
-        wa_raw = []
-        for h in range(2):
-            raw = sb(f"wa_raw{h}", [P, PACK, HALF], F32)
-            nc.sync.dma_start(raw[:], wa_rows[:, :, h * HALF : (h + 1) * HALF])
-            wa_raw.append(raw)
+        xw = sb("xw", [P, T], I32)
+        nc.sync.dma_start(xw[:], x_words[0].rearrange("p n t -> p (n t)").bitcast(I32))
+        nc.sync.dma_start(wa_raw[1][:], wa_rows[:, :, HALF:H])
         n1_t = load_list("n1_t", n1)
         n2_t = load_list("n2_t", n2)
         w1_raw = sb("w1_raw", [P, PACK, N], F32)
@@ -67,15 +73,14 @@ def tile_picked_tokkerngate_none_p_kernel(
         nc.sync.dma_start(gt_t[:], gt.rearrange("(p t) o -> p (t o)", t=PACK))
         n3_t = load_list("n3_t", n3)
 
-        xg_s = sb("xg_s", [P, S], U8)
-        nc.vector.tensor_copy(xg_s[:].rearrange("p (t m) -> p m t", t=PACK), xs[:].indirect(offs_t[:]))
-        xg_w = sb("xg_w", [P, S], U32)
-        nc.vector.tensor_copy(
-            xg_w[:].rearrange("p (t m) -> p m t", t=PACK), xw[:].bitcast(U32).indirect(offs_t[:])
-        )
+        ident = sb("ident", [P, P], F32)
+        make_identity(nc, ident[:])
+        minus_gt = sb("minus_gt", [P, PACK], F32)
+        nc.gpsimd.tensor_scalar(minus_gt[:], gt_t[:], -1.0, 0.0, ALU.mult, ALU.add)
 
-        wa_q = [sb(f"wa_q{h}", [P, HALF], U32) for h in range(2)]
-        wa_s = [sb(f"wa_s{h}", [P, HALF], U8) for h in range(2)]
+
+        wa_q = sb("wa_q", [P, H], U32)
+        wa_s = sb("wa_s", [P, H], U8)
 
         def cast_wa(engine, h, c0, width):
             grouped = sb(f"wa_g{h}_{c0}", [P, width * PACK], BF16)
@@ -89,121 +94,169 @@ def tile_picked_tokkerngate_none_p_kernel(
 
         def quant_wa(grouped, h, c0, width):
             nc.vector.quantize_mx(
-                out=wa_q[h][:, c0 : c0 + width].bitcast(FP8X4), scales=wa_s[h][:, c0 : c0 + width], in_=grouped[:]
+                out=wa_q[:, h * HALF + c0 : h * HALF + c0 + width].bitcast(FP8X4),
+                scales=wa_s[:, h * HALF + c0 : h * HALF + c0 + width],
+                in_=grouped[:],
             )
 
         y_ps = [psum.tile([P, H], F32, name=f"y_ps{t}", tag=f"bank{t}") for t in range(PACK)]
-        y_sb = [sb(f"y_sb{t}", [P, H], F32) for t in range(PACK)]
+        y_sb = [reuse.tile([P, H], F32, name=f"y_sb{t}", offset=t * H * 4) for t in range(PACK)]
 
-        def product_y(h):
-            cols = slice(h * HALF, (h + 1) * HALF)
-            for t in range(PACK):
+        def product_y(cols, tiles):
+            for t in tiles:
                 rows = slice(t * P, (t + 1) * P)
                 nc.tensor.matmul_mx(
                     out=y_ps[t][:, cols],
                     lhsT=xg_w[:, rows].bitcast(FP8X4),
                     lhsT_scale=xg_s[:, rows],
-                    rhs=wa_q[h][:].bitcast(FP8X4),
-                    rhs_scale=wa_s[h][:],
+                    rhs=wa_q[:, cols].bitcast(FP8X4),
+                    rhs_scale=wa_s[:, cols],
                     start=True,
                     stop=True,
                 )
 
-        def empty_y(engine, t, h):
-            cols = slice(h * HALF, (h + 1) * HALF)
+        def empty_y(engine, t, cols):
             if engine == "vector":
                 nc.vector.tensor_copy(y_sb[t][:, cols], y_ps[t][:, cols])
             else:
                 nc.scalar.copy(y_sb[t][:, cols], y_ps[t][:, cols])
 
-        g0 = cast_wa("scalar", 0, 0, HALF)
+        g0 = cast_wa("vector", 0, 0, HALF)
         quant_wa(g0, 0, 0, HALF)
+        xg_s = sb("xg_s", [P, S], U8)
+        nc.vector.tensor_copy(xg_s[:].rearrange("p (t m) -> p m t", t=PACK), xs[:].indirect(offs_t[:]))
+        xg_w = sb("xg_w", [P, S], U32)
+        nc.vector.tensor_copy(
+            xg_w[:].rearrange("p (t m) -> p m t", t=PACK), xw[:].bitcast(U32).indirect(offs_t[:])
+        )
+
         g2 = cast_wa("vector", 1, 0, CHUNK)
         g3 = cast_wa("scalar", 1, CHUNK, CHUNK)
-        product_y(0)
         quant_wa(g2, 1, 0, CHUNK)
         quant_wa(g3, 1, CHUNK, CHUNK)
-        for t in range(PACK):
-            empty_y("scalar", t, 0)
-        product_y(1)
-        empty_y("scalar", 0, 1)
-        empty_y("vector", 1, 1)
+        product_y(slice(0, HALF), (0, 1))
+        empty_y("scalar", 0, slice(0, HALF))
+        empty_y("scalar", 1, slice(0, HALF))
+        product_y(slice(HALF, H), (0, 1))
+        product_y(slice(0, H), (2, 3))
+        empty_y("scalar", 0, slice(HALF, H))
+        empty_y("vector", 1, slice(HALF, H))
 
         units = [(t, h) for h in range(2) for t in range(PACK)]
         pick = [sb(f"pick{u}", [P, 2, HALF], F32) for u in range(8)]
-        diff = [sb(f"diff{u}", [P, 2, HALF], F32) for u in range(8)]
-        sq_pair = [sb(f"sq{v}", [P, PACK * HALF], F32) for v in range(4)]
-        sq = [sq_pair[u // 2][:, (u % 2) * 2 * HALF : (u % 2 + 1) * 2 * HALF] for u in range(8)]
+        sq_pair = [sb(f"sq{v}", [P, PACK, HALF], F32) for v in range(4)]
+        sq = [sq_pair[u // 2][:, :, (u % 2) * CHUNK : (u % 2 + 1) * CHUNK] for u in range(8)]
         kt = [sb(f"kt{u}", [P, 2, 2, HALF], F32) for u in range(8)]
-        both = [sb(f"both{h}", [P, PACK, 2, HALF], F32) for h in range(2)]
+        both = sb("both", [P, PACK, 2, HALF], F32)
+        both_ps = {}
+        diff = {}
+        turned = {}
+
+        def transpose_sum(dst, parts):
+            for n, part in enumerate(parts):
+                nc.tensor.matmul(
+                    dst, part, ident[:], start=(n == 0), stop=(n == len(parts) - 1), is_transpose=True
+                )
 
         def fetch(u, engines):
             t, h = units[u]
             cols = slice(h * HALF, (h + 1) * HALF)
-            gather(engines[0], pick[u][:, 0, :], y_sb[t], n1_t, cols)
-            gather(engines[1], pick[u][:, 1, :], y_sb[t], n2_t, cols)
+            gather(engines[0], pick[u][:, 0, :], y_sb[t], n1_t, cols, negate=(h == 0))
+            gather(engines[1], pick[u][:, 1, :], y_sb[t], n2_t, cols, negate=(h == 0))
 
         def subtract(u):
             t, h = units[u]
-            cols = slice(h * HALF, (h + 1) * HALF)
-            nc.vector.tensor_tensor(
-                diff[u][:], pick[u][:], y_ps[t][:, cols].unsqueeze(1).to_broadcast([P, 2, HALF]), ALU.subtract
-            )
+            if h == 0:
+                diff[u] = psum.tile([P, 2, HALF], F32, name=f"diff{u}", tag=f"bank{PACK + t}")
+                for ab in range(2):
+                    for blk in (slice(0, P), slice(P, HALF)):
+                        transpose_sum(diff[u][:, ab, blk], [pick[u][:, ab, blk], y_sb[t][:, blk]])
+            else:
+                diff[u] = sb(f"diff{u}", [P, 2, HALF], F32)
+                nc.gpsimd.tensor_tensor(
+                    diff[u][:], pick[u][:], y_sb[t][:, HALF:H].unsqueeze(1).to_broadcast([P, 2, HALF]), ALU.subtract
+                )
+
+        def turn(u):
+            turned[u] = psum.tile([P, 2, HALF], F32, name=f"turned{u}", tag=f"bank{u}")
+            for ab in range(2):
+                for blk in (slice(0, P), slice(P, HALF)):
+                    transpose_sum(turned[u][:, ab, blk], [pick[u][:, ab, blk]])
 
         def weights(u):
-            nc.scalar.activation(sq[u], diff[u][:].rearrange("p a c -> p (a c)"), ACT.Square)
-            nc.scalar.activation(kt[u][:, 0].rearrange("p a c -> p (a c)"), sq[u], ACT.Exp, scale=-0.5)
+            nc.scalar.activation(sq[u], diff[u][:].rearrange("p a (b c) -> p (a b) c", c=CHUNK), ACT.Square)
+            nc.scalar.activation(
+                kt[u][:, 0].rearrange("p a (b c) -> p (a b) c", c=CHUNK), sq[u], ACT.Exp, scale=-0.5
+            )
 
         def sums(u):
             t, h = units[u]
-            nc.vector.scalar_tensor_tensor(
-                kt[u][:, 1].rearrange("p a c -> p (a c)"),
-                kt[u][:, 0].rearrange("p a c -> p (a c)"),
-                gt_t[:, t : t + 1],
-                pick[u][:].rearrange("p a c -> p (a c)"),
-                ALU.mult,
-                ALU.mult,
-            )
-            nc.vector.tensor_tensor(both[h][:, t], kt[u][:, :, 0, :], kt[u][:, :, 1, :], ALU.add)
+            if h == 0:
+                nc.vector.tensor_tensor(kt[u][:, 1], turned[u][:], kt[u][:, 0], ALU.mult)
+                both_ps[t] = psum.tile([P, 2, HALF], F32, name=f"both_ps{t}", tag=f"bank{t}")
+                for kind in range(2):
+                    for blk in (slice(0, P), slice(P, HALF)):
+                        transpose_sum(both_ps[t][:, kind, blk], [kt[u][:, kind, 0, blk], kt[u][:, kind, 1, blk]])
+            else:
+                nc.vector.scalar_tensor_tensor(
+                    kt[u][:, 1].rearrange("p a c -> p (a c)"),
+                    kt[u][:, 0].rearrange("p a c -> p (a c)"),
+                    gt_t[:, t : t + 1],
+                    pick[u][:].rearrange("p a c -> p (a c)"),
+                    ALU.mult,
+                    ALU.mult,
+                )
+                adder = nc.gpsimd if t == 0 else nc.vector
+                adder.tensor_tensor(both[:, t], kt[u][:, :, 0, :], kt[u][:, :, 1, :], ALU.add)
 
         w1_g = sb("w1_g", [P, N * PACK], BF16)
         w1_q = sb("w1_q", [P, N], U32)
         w1_s = sb("w1_s", [P, N], U8)
 
-        fetch(0, ("scalar", "scalar"))
-        fetch(1, ("vector", "vector"))
-        empty_y("vector", 2, 1)
-        empty_y("vector", 3, 1)
-        subtract(0)
-        fetch(2, ("scalar", "vector"))
-        subtract(1)
-        weights(0)
-        nc.vector.tensor_copy(
-            w1_g[:].rearrange("p (t m j) -> p m j t", t=PACK, j=PACK),
-            w1_raw[:].rearrange("p j (m t) -> p m j t", t=PACK),
-        )
-        for u in range(1, 8):
-            if u + 2 < 8:
-                fetch(u + 2, ("scalar", "vector" if u == 1 else "scalar"))
-            if u + 1 < 8:
-                subtract(u + 1)
+        def fetch_unit(u):
+            if u in (2, 3):
+                empty_y("scalar", u, slice(0, H))
+            fetch(u, ("scalar" if u < PACK else "vector", "vector"))
+
+        for t in range(PACK):
+            nc.gpsimd.tensor_scalar(
+                w1_g[:, t * N : (t + 1) * N].rearrange("p (m j) -> p m j", j=PACK),
+                w1_raw[:].rearrange("p j (m t) -> p t m j", t=PACK)[:, t],
+                1.0,
+                0.0,
+                ALU.mult,
+                ALU.add,
+            )
+        for u in range(8):
+            fetch_unit(u)
+        for u in range(8):
+            subtract(u)
+        for u in range(PACK):
+            turn(u)
+        nc.vector.quantize_mx(out=w1_q[:].bitcast(FP8X4), scales=w1_s[:], in_=w1_g[:])
+        for u in range(8):
             weights(u)
-            sums(u - 1)
-            if u == 1:
-                nc.vector.quantize_mx(out=w1_q[:].bitcast(FP8X4), scales=w1_s[:], in_=w1_g[:])
+            if u > 0:
+                sums(u - 1)
         sums(7)
 
-        h_ps = [
-            [psum.tile([P, H], F32, name=f"h_ps0_{t}", tag=f"bank{PACK + t}") for t in range(PACK)],
-            [psum.tile([P, H], F32, name=f"h_ps1_{t}", tag=f"bank{t}") for t in range(PACK)],
-        ]
         gate = [sb(f"gate{t}", [P, H], F32) for t in range(PACK)]
-        roots = []
-        for c in range(4):
-            h, c0 = c // 2, (c % 2) * CHUNK
-            root = sq_pair[3 - h][:].rearrange("p (t c) -> p t c", t=PACK)[:, :, c0 : c0 + CHUNK]
-            nc.scalar.activation(root, both[h][:, :, 0, c0 : c0 + CHUNK], ACT.Abs_reciprocal_sqrt, bias=0.5)
-            roots.append(root)
+        root = [sq_pair[3], sq_pair[2]]
+        once = [sb(f"once{h}", [P, PACK, HALF], F32) for h in range(2)]
+        for t in range(PACK):
+            nc.scalar.activation(root[0][:, t], both_ps[t][:, 0], ACT.Abs_reciprocal_sqrt, bias=0.5)
+        for cols in (slice(0, CHUNK), slice(CHUNK, HALF)):
+            nc.scalar.activation(root[1][:, :, cols], both[:, :, 0, cols], ACT.Abs_reciprocal_sqrt, bias=0.5)
+        for cols in (slice(0, CHUNK), slice(CHUNK, HALF)):
+            nc.scalar.activation(once[1][:, :, cols], root[1][:, :, cols], ACT.Square)
+        for t in range(PACK):
+            nc.vector.scalar_tensor_tensor(
+                once[0][:, t], both_ps[t][:, 1], minus_gt[:, t : t + 1], root[0][:, t], ALU.mult, ALU.mult
+            )
+        h_ps = [
+            [psum.tile([P, H], F32, name=f"h_ps{h}_{t}", tag=f"bank{PACK * h + t}") for t in range(PACK)]
+            for h in range(2)
+        ]
 
         def sigmoid_h(h, c0, width):
             for t in range(PACK):
@@ -211,18 +264,12 @@ def tile_picked_tokkerngate_none_p_kernel(
                     gate[t][:, h * HALF + c0 : h * HALF + c0 + width], h_ps[h][t][:, c0 : c0 + width], ACT.Sigmoid
                 )
 
-        def scale_once(c):
-            h, c0 = c // 2, (c % 2) * CHUNK
-            once = sb(f"once{c}", [P, PACK, CHUNK], F32)
-            nc.vector.tensor_tensor(once[:], both[h][:, :, 1, c0 : c0 + CHUNK], roots[c], ALU.mult)
-            return once
-
-        def scale_twice(c, once):
+        def form_z(c, pair):
             z = sb(f"z{c}", [P, CHUNK * PACK], BF16)
             nc.vector.tensor_tensor(
                 z[:].rearrange("p (c i t) -> p c t i", i=4, t=PACK),
-                once[:].rearrange("p t (c i) -> p c t i", i=4),
-                roots[c].rearrange("p t (c i) -> p c t i", i=4),
+                pair[0].rearrange("p t (c i) -> p c t i", i=4),
+                pair[1].rearrange("p t (c i) -> p c t i", i=4),
                 ALU.mult,
             )
             return z
@@ -244,23 +291,29 @@ def tile_picked_tokkerngate_none_p_kernel(
                     stop=True,
                 )
 
-        once = scale_once(0)
-        for c in range(4):
-            z = scale_twice(c, once)
-            if c + 1 < 4:
-                once = scale_once(c + 1)
-            product_h(c, z)
-            if c == 1:
-                sigmoid_h(0, 0, HALF)
-            if c >= 2:
-                sigmoid_h(1, (c - 2) * CHUNK, CHUNK)
+        pairs = [
+            (once[h][:, :, cols], root[0][:, :, cols] if h == 0 else both[:, :, 1, cols])
+            for h in range(2)
+            for cols in (slice(0, CHUNK), slice(CHUNK, HALF))
+        ]
+        for h in range(2):
+            zs = [form_z(c, pairs[c]) for c in (2 * h, 2 * h + 1)]
+            for c in (2 * h, 2 * h + 1):
+                product_h(c, zs[c - 2 * h])
+            sigmoid_h(h, 0, HALF)
+        h_sb = [sb(f"h_sb{t}", [P, HALF], F32) for t in range(PACK)]
+        for t in range(PACK):
+            nc.vector.tensor_copy(h_sb[t][:], h_ps[0][t][:, 0:HALF])
 
         out_rows = out.rearrange("(p t) c -> p t c", t=PACK)
         for t in range(PACK):
             for h in range(2):
                 cols = slice(h * HALF, (h + 1) * HALF)
                 fetched = sb(f"fetched{t}_{h}", [P, HALF], F32)
-                gather("vector" if t == 0 else "scalar", fetched[:], gate[t], n3_t, cols)
+                gather("vector" if h == 0 else "scalar", fetched[:], gate[t], n3_t, cols)
                 res = sb(f"res{t}_{h}", [P, HALF], F32)
-                nc.vector.tensor_tensor(res[:], h_ps[h][t][:, 0:HALF], fetched[:], ALU.mult)
+                if h == 0:
+                    nc.gpsimd.tensor_tensor(res[:], h_sb[t][:], fetched[:], ALU.mult)
+                else:
+                    nc.vector.tensor_tensor(res[:], h_ps[1][t][:, 0:HALF], fetched[:], ALU.mult)
                 nc.sync.dma_start(out_rows[:, t, cols], res[:])

from contextlib import ExitStack

import concourse.mybir as mybir
from concourse.masks import make_identity

K, T, S, N, H = 512, 2048, 512, 512, 512
FLOPS = 2 * K * S * H + 2 * S * N * H

F32 = mybir.dt.float32
BF16 = mybir.dt.bfloat16
I32 = mybir.dt.int32
U32 = mybir.dt.uint32
U16 = mybir.dt.uint16
U8 = mybir.dt.uint8
FP8X4 = mybir.dt.float8_e4m3fn_x4
ACT = mybir.ActivationFunctionType
ALU = mybir.AluOpType

P = 128
PACK = 4
HALF = 256
CHUNK = 128


def tile_picked_tokkerngate_none_p_kernel(
    tc, x_words, x_scales, wa, gt, w1, offs, n1, n2, n3, out
):
    nc = tc.nc
    with ExitStack() as ctx:
        keep = ctx.enter_context(tc.tile_pool(name="keep", bufs=1))
        reuse = ctx.enter_context(tc.tile_pool(name="reuse", bufs=1))
        psum = ctx.enter_context(tc.psum_pool(name="psum", bufs=1))

        def sb(name, shape, dtype):
            return keep.tile(shape, dtype, name=name, align_bytes=64)

        def load_list(name, src):
            tile = keep.tile([P, 32], U16, name=name)
            nc.sync.dma_start(tile[:], src)
            return tile

        def gather(engine, dst, window, lst, cols, negate=False):
            src = window[:].indirect(lst[:, cols.start // 16 : cols.stop // 16])
            if engine == "vector" and negate:
                nc.vector.tensor_scalar(dst, src, -1.0, 0.0, ALU.mult, ALU.add)
            elif engine == "vector":
                nc.vector.tensor_copy(dst, src)
            else:
                nc.scalar.activation(dst, src, ACT.Copy, scale=-1.0 if negate else 1.0)

        wa_rows = wa.rearrange("(p j) c -> p j c", j=PACK)
        wa_raw = [
            sb("wa_raw0", [P, PACK, HALF], F32),
            reuse.tile([P, PACK, HALF], F32, name="wa_raw1", offset=0),
        ]
        nc.sync.dma_start(wa_raw[0][:], wa_rows[:, :, 0:HALF])
        offs_t = load_list("offs_t", offs)
        xs = sb("xs", [P, T], U8)
        nc.vector.memset(xs[:, 0 : T // 2].bitcast(I32), 0)
        nc.gpsimd.memset(xs[:, T // 2 : T].bitcast(I32), 0)
        for q in range(4):
            nc.sync.dma_start(
                xs[32 * q : 32 * q + 4, :].bitcast(I32), x_scales[0, 4 * q : 4 * q + 4, :].bitcast(I32)
            )
        xw = sb("xw", [P, T], I32)
        nc.sync.dma_start(xw[:], x_words[0].rearrange("p n t -> p (n t)").bitcast(I32))
        nc.sync.dma_start(wa_raw[1][:], wa_rows[:, :, HALF:H])
        n1_t = load_list("n1_t", n1)
        n2_t = load_list("n2_t", n2)
        w1_raw = sb("w1_raw", [P, PACK, N], F32)
        nc.sync.dma_start(w1_raw[:], w1.rearrange("(p j) c -> p j c", j=PACK))
        gt_t = sb("gt_t", [P, PACK], F32)
        nc.sync.dma_start(gt_t[:], gt.rearrange("(p t) o -> p (t o)", t=PACK))
        n3_t = load_list("n3_t", n3)

        ident = sb("ident", [P, P], F32)
        make_identity(nc, ident[:])
        minus_gt = sb("minus_gt", [P, PACK], F32)
        nc.gpsimd.tensor_scalar(minus_gt[:], gt_t[:], -1.0, 0.0, ALU.mult, ALU.add)


        wa_q = sb("wa_q", [P, H], U32)
        wa_s = sb("wa_s", [P, H], U8)

        def cast_wa(engine, h, c0, width):
            grouped = sb(f"wa_g{h}_{c0}", [P, width * PACK], BF16)
            dst = grouped[:].rearrange("p (c i j) -> p c j i", i=4, j=PACK)
            src = wa_raw[h][:, :, c0 : c0 + width].rearrange("p j (c i) -> p c j i", i=4)
            if engine == "vector":
                nc.vector.tensor_copy(dst, src)
            else:
                nc.scalar.copy(dst, src)
            return grouped

        def quant_wa(grouped, h, c0, width):
            nc.vector.quantize_mx(
                out=wa_q[:, h * HALF + c0 : h * HALF + c0 + width].bitcast(FP8X4),
                scales=wa_s[:, h * HALF + c0 : h * HALF + c0 + width],
                in_=grouped[:],
            )

        y_ps = [psum.tile([P, H], F32, name=f"y_ps{t}", tag=f"bank{t}") for t in range(PACK)]
        y_sb = [reuse.tile([P, H], F32, name=f"y_sb{t}", offset=t * H * 4) for t in range(PACK)]

        def product_y(cols, tiles):
            for t in tiles:
                rows = slice(t * P, (t + 1) * P)
                nc.tensor.matmul_mx(
                    out=y_ps[t][:, cols],
                    lhsT=xg_w[:, rows].bitcast(FP8X4),
                    lhsT_scale=xg_s[:, rows],
                    rhs=wa_q[:, cols].bitcast(FP8X4),
                    rhs_scale=wa_s[:, cols],
                    start=True,
                    stop=True,
                )

        def empty_y(engine, t, cols):
            if engine == "vector":
                nc.vector.tensor_copy(y_sb[t][:, cols], y_ps[t][:, cols])
            else:
                nc.scalar.copy(y_sb[t][:, cols], y_ps[t][:, cols])

        g0 = cast_wa("vector", 0, 0, HALF)
        quant_wa(g0, 0, 0, HALF)
        xg_s = sb("xg_s", [P, S], U8)
        nc.vector.tensor_copy(xg_s[:].rearrange("p (t m) -> p m t", t=PACK), xs[:].indirect(offs_t[:]))
        xg_w = sb("xg_w", [P, S], U32)
        nc.vector.tensor_copy(
            xg_w[:].rearrange("p (t m) -> p m t", t=PACK), xw[:].bitcast(U32).indirect(offs_t[:])
        )

        g2 = cast_wa("vector", 1, 0, CHUNK)
        g3 = cast_wa("scalar", 1, CHUNK, CHUNK)
        quant_wa(g2, 1, 0, CHUNK)
        quant_wa(g3, 1, CHUNK, CHUNK)
        product_y(slice(0, HALF), (0, 1))
        empty_y("scalar", 0, slice(0, HALF))
        empty_y("scalar", 1, slice(0, HALF))
        product_y(slice(HALF, H), (0, 1))
        product_y(slice(0, H), (2, 3))
        empty_y("scalar", 0, slice(HALF, H))
        empty_y("vector", 1, slice(HALF, H))

        units = [(t, h) for h in range(2) for t in range(PACK)]
        pick = [sb(f"pick{u}", [P, 2, HALF], F32) for u in range(8)]
        sq_pair = [sb(f"sq{v}", [P, PACK, HALF], F32) for v in range(4)]
        sq = [sq_pair[u // 2][:, :, (u % 2) * CHUNK : (u % 2 + 1) * CHUNK] for u in range(8)]
        kt = [sb(f"kt{u}", [P, 2, 2, HALF], F32) for u in range(8)]
        both = sb("both", [P, PACK, 2, HALF], F32)
        both_ps = {}
        diff = {}
        turned = {}

        def transpose_sum(dst, parts):
            for n, part in enumerate(parts):
                nc.tensor.matmul(
                    dst, part, ident[:], start=(n == 0), stop=(n == len(parts) - 1), is_transpose=True
                )

        def fetch(u, engines):
            t, h = units[u]
            cols = slice(h * HALF, (h + 1) * HALF)
            gather(engines[0], pick[u][:, 0, :], y_sb[t], n1_t, cols, negate=(h == 0))
            gather(engines[1], pick[u][:, 1, :], y_sb[t], n2_t, cols, negate=(h == 0))

        def subtract(u):
            t, h = units[u]
            if h == 0:
                diff[u] = psum.tile([P, 2, HALF], F32, name=f"diff{u}", tag=f"bank{PACK + t}")
                for ab in range(2):
                    for blk in (slice(0, P), slice(P, HALF)):
                        transpose_sum(diff[u][:, ab, blk], [pick[u][:, ab, blk], y_sb[t][:, blk]])
            else:
                diff[u] = sb(f"diff{u}", [P, 2, HALF], F32)
                nc.gpsimd.tensor_tensor(
                    diff[u][:], pick[u][:], y_sb[t][:, HALF:H].unsqueeze(1).to_broadcast([P, 2, HALF]), ALU.subtract
                )

        def turn(u):
            turned[u] = psum.tile([P, 2, HALF], F32, name=f"turned{u}", tag=f"bank{u}")
            for ab in range(2):
                for blk in (slice(0, P), slice(P, HALF)):
                    transpose_sum(turned[u][:, ab, blk], [pick[u][:, ab, blk]])

        def weights(u):
            nc.scalar.activation(sq[u], diff[u][:].rearrange("p a (b c) -> p (a b) c", c=CHUNK), ACT.Square)
            nc.scalar.activation(
                kt[u][:, 0].rearrange("p a (b c) -> p (a b) c", c=CHUNK), sq[u], ACT.Exp, scale=-0.5
            )

        def sums(u):
            t, h = units[u]
            if h == 0:
                nc.vector.tensor_tensor(kt[u][:, 1], turned[u][:], kt[u][:, 0], ALU.mult)
                both_ps[t] = psum.tile([P, 2, HALF], F32, name=f"both_ps{t}", tag=f"bank{t}")
                for kind in range(2):
                    for blk in (slice(0, P), slice(P, HALF)):
                        transpose_sum(both_ps[t][:, kind, blk], [kt[u][:, kind, 0, blk], kt[u][:, kind, 1, blk]])
            else:
                nc.vector.scalar_tensor_tensor(
                    kt[u][:, 1].rearrange("p a c -> p (a c)"),
                    kt[u][:, 0].rearrange("p a c -> p (a c)"),
                    gt_t[:, t : t + 1],
                    pick[u][:].rearrange("p a c -> p (a c)"),
                    ALU.mult,
                    ALU.mult,
                )
                adder = nc.gpsimd if t == 0 else nc.vector
                adder.tensor_tensor(both[:, t], kt[u][:, :, 0, :], kt[u][:, :, 1, :], ALU.add)

        w1_g = sb("w1_g", [P, N * PACK], BF16)
        w1_q = sb("w1_q", [P, N], U32)
        w1_s = sb("w1_s", [P, N], U8)

        def fetch_unit(u):
            if u in (2, 3):
                empty_y("scalar", u, slice(0, H))
            fetch(u, ("scalar" if u < PACK else "vector", "vector"))

        for t in range(PACK):
            nc.gpsimd.tensor_scalar(
                w1_g[:, t * N : (t + 1) * N].rearrange("p (m j) -> p m j", j=PACK),
                w1_raw[:].rearrange("p j (m t) -> p t m j", t=PACK)[:, t],
                1.0,
                0.0,
                ALU.mult,
                ALU.add,
            )
        for u in range(8):
            fetch_unit(u)
        for u in range(8):
            subtract(u)
        for u in range(PACK):
            turn(u)
        nc.vector.quantize_mx(out=w1_q[:].bitcast(FP8X4), scales=w1_s[:], in_=w1_g[:])
        for u in range(8):
            weights(u)
            if u > 0:
                sums(u - 1)
        sums(7)

        gate = [sb(f"gate{t}", [P, H], F32) for t in range(PACK)]
        root = [sq_pair[3], sq_pair[2]]
        once = [sb(f"once{h}", [P, PACK, HALF], F32) for h in range(2)]
        for t in range(PACK):
            nc.scalar.activation(root[0][:, t], both_ps[t][:, 0], ACT.Abs_reciprocal_sqrt, bias=0.5)
        for cols in (slice(0, CHUNK), slice(CHUNK, HALF)):
            nc.scalar.activation(root[1][:, :, cols], both[:, :, 0, cols], ACT.Abs_reciprocal_sqrt, bias=0.5)
        for cols in (slice(0, CHUNK), slice(CHUNK, HALF)):
            nc.scalar.activation(once[1][:, :, cols], root[1][:, :, cols], ACT.Square)
        for t in range(PACK):
            nc.vector.scalar_tensor_tensor(
                once[0][:, t], both_ps[t][:, 1], minus_gt[:, t : t + 1], root[0][:, t], ALU.mult, ALU.mult
            )
        h_ps = [
            [psum.tile([P, H], F32, name=f"h_ps{h}_{t}", tag=f"bank{PACK * h + t}") for t in range(PACK)]
            for h in range(2)
        ]

        def sigmoid_h(h, c0, width):
            for t in range(PACK):
                nc.scalar.activation(
                    gate[t][:, h * HALF + c0 : h * HALF + c0 + width], h_ps[h][t][:, c0 : c0 + width], ACT.Sigmoid
                )

        def form_z(c, pair):
            z = sb(f"z{c}", [P, CHUNK * PACK], BF16)
            nc.vector.tensor_tensor(
                z[:].rearrange("p (c i t) -> p c t i", i=4, t=PACK),
                pair[0].rearrange("p t (c i) -> p c t i", i=4),
                pair[1].rearrange("p t (c i) -> p c t i", i=4),
                ALU.mult,
            )
            return z

        def product_h(c, z):
            h, c0 = c // 2, (c % 2) * CHUNK
            z_q = sb(f"z_q{c}", [P, CHUNK], U32)
            z_s = sb(f"z_s{c}", [P, CHUNK], U8)
            nc.vector.quantize_mx(out=z_q[:].bitcast(FP8X4), scales=z_s[:], in_=z[:])
            for t in range(PACK):
                rows = slice(t * P, (t + 1) * P)
                nc.tensor.matmul_mx(
                    out=h_ps[h][t][:, c0 : c0 + CHUNK],
                    lhsT=w1_q[:, rows].bitcast(FP8X4),
                    lhsT_scale=w1_s[:, rows],
                    rhs=z_q[:].bitcast(FP8X4),
                    rhs_scale=z_s[:],
                    start=True,
                    stop=True,
                )

        pairs = [
            (once[h][:, :, cols], root[0][:, :, cols] if h == 0 else both[:, :, 1, cols])
            for h in range(2)
            for cols in (slice(0, CHUNK), slice(CHUNK, HALF))
        ]
        for h in range(2):
            zs = [form_z(c, pairs[c]) for c in (2 * h, 2 * h + 1)]
            for c in (2 * h, 2 * h + 1):
                product_h(c, zs[c - 2 * h])
            sigmoid_h(h, 0, HALF)
        h_sb = [sb(f"h_sb{t}", [P, HALF], F32) for t in range(PACK)]
        for t in range(PACK):
            nc.vector.tensor_copy(h_sb[t][:], h_ps[0][t][:, 0:HALF])

        out_rows = out.rearrange("(p t) c -> p t c", t=PACK)
        for t in range(PACK):
            for h in range(2):
                cols = slice(h * HALF, (h + 1) * HALF)
                fetched = sb(f"fetched{t}_{h}", [P, HALF], F32)
                gather("vector" if h == 0 else "scalar", fetched[:], gate[t], n3_t, cols)
                res = sb(f"res{t}_{h}", [P, HALF], F32)
                if h == 0:
                    nc.gpsimd.tensor_tensor(res[:], h_sb[t][:], fetched[:], ALU.mult)
                else:
                    nc.vector.tensor_tensor(res[:], h_ps[1][t][:, 0:HALF], fetched[:], ALU.mult)
                nc.sync.dma_start(out_rows[:, t, cols], res[:])
